import numpy as np
import ml_dtypes


def mxq(x, axis, fmt="e4m3"):
    dtype, down = {"e4m3": (ml_dtypes.float8_e4m3fn, 7), "e5m2": (ml_dtypes.float8_e5m2, 14)}[fmt]
    v = np.moveaxis(np.asarray(x, np.float32).astype(ml_dtypes.bfloat16).astype(np.float64), axis, -1)
    blocks = v.reshape(v.shape[:-1] + (-1, 32))
    amax = np.abs(blocks).max(-1, keepdims=True)
    byte = np.maximum(np.where(amax > 0, np.frexp(amax)[1] - 1 + 127, 0) - down, 1)
    scale = np.exp2(byte - 127.0)
    codes = (blocks / scale).astype(np.float32).astype(dtype).astype(np.float64)
    return np.moveaxis((codes * scale).reshape(v.shape), -1, axis)


WIDE = False


def mx_kscale(k):
    if not WIDE:
        return np.ones(k)
    levels = np.array([10, -10, 5, -5, 0])
    if k % 512:
        return np.exp2(np.random.permutation(np.resize(levels, k // 32))).repeat(32)
    a = np.empty((k // 512, 16))
    for p in range(k // 512):
        a[p, :8] = np.random.permutation(np.resize(levels, 8))
        for g in range(8):
            far = levels[np.abs(levels - a[p, g]) >= 10]
            a[p, g + 8] = far[np.random.randint(len(far))]
    return np.exp2(a.ravel()).repeat(32)


def f64(x):
    return np.asarray(x).astype(np.float64)


E2M1 = np.array([0.0, 0.5, 1.0, 1.5, 2.0, 3.0, 4.0, 6.0, -0.0, -0.5, -1.0, -1.5, -2.0, -3.0, -4.0, -6.0])


def pack_weight(w, fmt):
    k, n = w.shape
    w = f64(np.asarray(w, np.float32).astype(ml_dtypes.bfloat16)).reshape(k // 32, 32, n)
    amax = np.abs(w).max(1)
    if fmt == "e4m3":
        byte = np.frexp(amax)[1] - 1 + 127 - 7
    else:
        mant, ex = np.frexp(amax / 6.0)
        byte = np.where(mant > 0.5, ex, ex - 1) + 127
    byte = np.clip(np.where(amax > 0, byte, 1), 1, 254)
    scaled = (w * np.exp2(127.0 - byte)[:, None, :]).reshape(k, n).astype(np.float32)
    by_word = np.ascontiguousarray(scaled.reshape(k // 512, 128, 4, n).transpose(0, 1, 3, 2))
    if fmt == "e4m3":
        words = by_word.astype(ml_dtypes.float8_e4m3fn).view(np.uint8)
    else:
        c = by_word.astype(ml_dtypes.float4_e2m1fn).view(np.uint8) & 0xF
        words = (c[..., 0::2] | (c[..., 1::2] << 4)).reshape(k // 512, 128, 2 * n)
    return np.ascontiguousarray(words), np.ascontiguousarray(byte.astype(np.uint8).reshape(k // 512, 16, n))


def unpack_weight(words, scales, fmt):
    g, _, n = scales.shape
    words = np.ascontiguousarray(words).reshape(g, 128, n, -1)
    if fmt == "e4m3":
        vals = words.view(ml_dtypes.float8_e4m3fn).astype(np.float64)
    else:
        nib = np.empty((g, 128, n, 4), np.uint8)
        nib[..., 0::2] = words & 0xF
        nib[..., 1::2] = words >> 4
        vals = E2M1[nib]
    vals = vals * np.repeat(np.exp2(scales.astype(np.float64) - 127.0), 8, axis=1)[..., None]
    return vals.transpose(0, 1, 3, 2).reshape(g * 512, n)


def bf(x):
    return np.asarray(x, np.float32).astype(ml_dtypes.bfloat16)


def planes(Y):
    r, m = Y.shape
    b = f64(bf(Y)).reshape(r // 32, 32, m)
    amax = np.abs(b).max(1)
    byte = np.clip(np.where(amax > 0, np.frexp(amax)[1] - 1 + 127 - 7, 1), 1, 254)
    codes = (b * np.exp2(127.0 - byte)[:, None, :]).reshape(r, m).astype(np.float32).astype(ml_dtypes.float8_e4m3fn).view(np.uint8)
    words = codes.reshape(r // 512, 128, 4, m).transpose(0, 1, 3, 2)
    return np.ascontiguousarray(words), np.ascontiguousarray(byte.astype(np.uint8).reshape(r // 512, 16, m))


K, T, S, N, M = 1024, 512, 512, 512, 512


def setup_inputs():
    n = np.random.standard_normal
    fk = mx_kscale(K)
    ft = mx_kscale(T)
    fs = mx_kscale(S)
    xtp = pack_weight(n((K, T)) / fk[:, None], "e2m1")
    wap = pack_weight(n((K, N)) * 1 / np.sqrt(K) * fk[:, None], "e4m3")
    wbp = pack_weight(n((K, M)) * 1 / np.sqrt(K) * fk[:, None], "e2m1")
    sap = pack_weight(n((S, N)) * fs[:, None], "e4m3")
    sbp = pack_weight(n((S, M)) / fs[:, None], "e2m1")
    return {
        "xt_words": xtp[0],
        "xt_scales": xtp[1],
        "wa_words": wap[0],
        "wa_scales": wap[1],
        "wb_words": wbp[0],
        "wb_scales": wbp[1],
        "ra": (np.random.uniform(0.5, 1.5, (1, T)) * ft).astype(np.float32),
        "rb": (np.random.uniform(0.5, 1.5, (1, T)) / ft).astype(np.float32),
        "sa_words": sap[0],
        "sa_scales": sap[1],
        "sb_words": sbp[0],
        "sb_scales": sbp[1],
    }


def reference(xt_words, xt_scales, wa_words, wa_scales, wb_words, wb_scales, ra, rb, sa_words, sa_scales, sb_words, sb_scales):
    xtu = unpack_weight(xt_words, xt_scales, "e2m1")
    wau = unpack_weight(wa_words, wa_scales, "e4m3")
    wbu = unpack_weight(wb_words, wb_scales, "e2m1")
    sau = unpack_weight(sa_words, sa_scales, "e4m3")
    sbu = unpack_weight(sb_words, sb_scales, "e2m1")
    a = wau.T @ xtu
    b = wbu.T @ xtu
    aw = np.maximum(a, 0.0) * f64(ra)
    bw = b * f64(rb)
    at = aw.T
    bt = bw.T
    atq = mxq(at, 0, "e4m3")
    btq = mxq(bt, 0, "e4m3")
    v = atq.T @ btq + sau.T @ sbu
    y = 0.04 * v
    words, scales = planes(y)
    return y, words, scales

@@ -1,0 +1,289 @@
+from contextlib import ExitStack
+
+import concourse.mybir as mybir
+
+K, T, S, N, M = 1024, 512, 512, 512, 512
+FLOPS = 2 * K * T * (N + M) + 2 * (T + S) * N * M
+
+F32 = mybir.dt.float32
+BF16 = mybir.dt.bfloat16
+I32 = mybir.dt.int32
+U32 = mybir.dt.uint32
+U8 = mybir.dt.uint8
+FP8X4 = mybir.dt.float8_e4m3fn_x4
+FP4X4 = mybir.dt.float4_e2m1fn_x4
+ALU = mybir.AluOpType
+ACT = mybir.ActivationFunctionType
+
+P = 128
+PACK = 4
+PASSES = 2
+CHUNK = 128
+OUT_SCALE = 0.04
+
+
+def tile_mix_moment_of_two_layers_pl_kernel(
+    tc, xt_words, xt_scales, wa_words, wa_scales, wb_words, wb_scales, ra, rb,
+    sa_words, sa_scales, sb_words, sb_scales, out_0, out_1, out_2,
+):
+    nc = tc.nc
+    with ExitStack() as ctx:
+        sb = ctx.enter_context(tc.tile_pool(name="sb", bufs=1))
+        ps = ctx.enter_context(tc.psum_pool(name="ps", bufs=1))
+        ctx.enter_context(tc.manual_schedule())
+
+        def sbuf(name, shape, dtype):
+            return sb.tile(shape, dtype, name=name, align_bytes=64)
+
+        banks = [ps.tile([P, 512], F32, name="bank%d" % i) for i in range(8)]
+        a_banks = banks[0:4]
+        b_banks = banks[4:8]
+        v_banks = banks[0:4]
+
+        xt_raw = sbuf("xt_raw", [P, PASSES, 2 * T], U8)
+        xt_raw_plane = sbuf("xt_raw_plane", [P, PASSES, T], U8)
+        xt_codes = [sbuf("xt_codes%d" % g, [P, 2 * T], U8) for g in range(PASSES)]
+        xt_plane = [sbuf("xt_plane%d" % g, [P, T], U8) for g in range(PASSES)]
+        wa_codes = [sbuf("wa_codes%d" % h, [P, PASSES, N // 2], U32) for h in range(2)]
+        wa_plane = sbuf("wa_plane", [P, PASSES, N], U8)
+        wb_codes = sbuf("wb_codes", [P, PASSES, 2 * M], U8)
+        wb_plane = sbuf("wb_plane", [P, PASSES, M], U8)
+        sa_raw = sbuf("sa_raw", [P, N], U32)
+        sa_raw_plane = sbuf("sa_raw_plane", [P, 1, N], U8)
+        sa_codes = sbuf("sa_codes", [P, N], U32)
+        sa_plane = sbuf("sa_plane", [P, N], U8)
+        sb_codes = sbuf("sb_codes", [P, 2 * M], U8)
+        sb_plane = sbuf("sb_plane", [P, 1, M], U8)
+        weight_rows = sbuf("weight_rows", [P, 32], F32)
+        weight_cols = sbuf("weight_cols", [P, 32], F32)
+        weights = sbuf("weights", [P, 2, PACK], F32)
+        at_bf = sbuf("at_bf", [P, PACK, P, PACK], BF16)
+        at_codes = sbuf("at_codes", [P, N], U32)
+        at_plane = sbuf("at_plane", [P, N], U8)
+        bt_bf = [sbuf("bt_bf%d" % c, [P, CHUNK, PACK], BF16) for c in range(4)]
+        bt_codes = sbuf("bt_codes", [P, M], U32)
+        bt_plane = sbuf("bt_plane", [P, M], U8)
+        y_f32 = [sbuf("y_f32_%d" % c, [P, PACK, CHUNK], F32) for c in range(4)]
+        y_bf = [sbuf("y_bf%d" % c, [P, CHUNK, PACK], BF16) for c in range(4)]
+        y_codes = sbuf("y_codes", [P, M], U32)
+        y_plane = sbuf("y_plane", [P, M], U8)
+
+        def zero_plane(plane):
+            nc.vector.memset(plane[:].rearrange("p g c -> p (g c)").bitcast(I32), 0)
+
+        def load_scale_rows(queue, plane, scales, q):
+            queue.dma_start(
+                out=plane[32 * q : 32 * q + 4, :, :].bitcast(I32),
+                in_=scales.bitcast(I32)[:, 4 * q : 4 * q + 4, :].rearrange("g r c -> r g c"),
+            )
+
+        def load_plane(plane, scales):
+            for q in range(4):
+                load_scale_rows(nc.sync if q % 2 == 0 else nc.scalar, plane, scales, q)
+
+        def load_weight_row(row, vector):
+            nc.scalar.dma_start(
+                out=weight_rows[row:P:8, :].rearrange("u (q i) -> u q i", i=8),
+                in_=vector.rearrange("o (q u i) -> u (o q) i", u=16, i=8),
+            )
+
+        def load_wa_half(h):
+            words = wa_words.rearrange("g p c t -> p g (c t)").bitcast(I32)
+            nc.sync.dma_start(out=wa_codes[h][:].bitcast(I32), in_=words[:, :, 256 * h : 256 * (h + 1)])
+
+        nc.vector.memset(weight_rows[:], 0.0)
+        for plane in (sa_raw_plane, wa_plane):
+            zero_plane(plane)
+        for g in range(PASSES):
+            nc.vector.memset(xt_plane[g][:].bitcast(I32), 0)
+        for plane in (wb_plane, sb_plane):
+            zero_plane(plane)
+
+        load_plane(xt_raw_plane, xt_scales)
+        nc.sync.dma_start(out=xt_raw[:].bitcast(I32), in_=xt_words.rearrange("g p c -> p g c").bitcast(I32))
+        load_wa_half(0)
+        load_weight_row(0, ra)
+        load_weight_row(1, rb)
+        for q in range(2, 4):
+            load_scale_rows(nc.gpsimd, sa_raw_plane, sa_scales, q)
+        load_plane(wa_plane, wa_scales)
+        load_wa_half(1)
+        nc.sync.dma_start(out=sa_raw[:].bitcast(I32), in_=sa_words[0].rearrange("p c t -> p (c t)").bitcast(I32))
+        for q in range(2):
+            load_scale_rows(nc.scalar, sa_raw_plane, sa_scales, q)
+        load_plane(wb_plane, wb_scales)
+        nc.sync.dma_start(out=wb_codes[:].bitcast(I32), in_=wb_words.rearrange("g p c -> p g c").bitcast(I32))
+        nc.sync.dma_start(out=sb_codes[:].bitcast(I32), in_=sb_words[0].bitcast(I32))
+        for q in range(4):
+            load_scale_rows(nc.scalar if q < 2 else nc.sync, sb_plane, sb_scales, q)
+
+        for g in range(PASSES):
+            for q in range(4):
+                rows = slice(32 * q, 32 * q + 4)
+                nc.vector.tensor_copy(
+                    out=xt_plane[g][rows, :].bitcast(I32).rearrange("p (j b q w) -> p j b q w", j=4, b=4, q=4),
+                    in_=xt_raw_plane[rows, g, :].bitcast(I32).rearrange("p (q b j w) -> p j b q w", q=4, b=4, j=4),
+                )
+        for g in range(PASSES):
+            nc.vector.tensor_copy(
+                out=xt_codes[g][:].bitcast(I32).rearrange("p (j b q w) -> p j b q w", j=4, b=4, q=4),
+                in_=xt_raw[:, g, :].bitcast(I32).rearrange("p (q b j w) -> p j b q w", q=4, b=4, j=4),
+            )
+        nc.vector.transpose(out=weight_cols[:], in_=weight_rows[:])
+
+        def layer_group(out, j, codes_of, plane, first, width):
+            for g in range(PASSES):
+                nc.tensor.matmul_mx(
+                    out=out,
+                    lhsT=xt_codes[g][:, 2 * P * j : 2 * P * (j + 1)].bitcast(FP4X4),
+                    lhsT_scale=xt_plane[g][:, P * j : P * (j + 1)],
+                    rhs=codes_of(g, first, width),
+                    rhs_scale=plane[:, g, first : first + width],
+                    start=(g == 0),
+                    stop=(g == PASSES - 1),
+                )
+
+        def wa_view(g, first, width):
+            h, column = divmod(first, N // 2)
+            return wa_codes[h][:, g, column : column + width].bitcast(FP8X4)
+
+        def wb_view(g, first, width):
+            return wb_codes[:, g, 2 * first : 2 * (first + width)].bitcast(FP4X4)
+
+        def a_chunk(c):
+            for j in range(PACK):
+                layer_group(a_banks[c][:, CHUNK * j : CHUNK * (j + 1)], j, wa_view, wa_plane, CHUNK * c, CHUNK)
+            sums = a_banks[c][:].rearrange("p (j q r) -> p r q j", j=PACK, r=PACK)
+            for r in range(PACK):
+                nc.vector.scalar_tensor_tensor(
+                    out=at_bf[:, r, 32 * c : 32 * (c + 1), :],
+                    in0=sums[:, r, :, :],
+                    scalar=0.0,
+                    in1=weights[:, 0:1, :].to_broadcast([P, 32, PACK]),
+                    op0=ALU.max,
+                    op1=ALU.mult,
+                )
+
+        def b_matmuls(c):
+            for j in range(PACK):
+                layer_group(b_banks[c][:, CHUNK * j : CHUNK * (j + 1)], j, wb_view, wb_plane, CHUNK * c, CHUNK)
+
+        def b_weigh_on_vector(c):
+            nc.vector.tensor_tensor(
+                out=bt_bf[c][:],
+                in0=b_banks[c][:].rearrange("p (j m) -> p m j", j=PACK),
+                in1=weights[:, 1:2, :].to_broadcast([P, CHUNK, PACK]),
+                op=ALU.mult,
+            )
+
+        def b_weigh_on_scalar(c):
+            for j in range(PACK):
+                nc.scalar.activation(
+                    out=bt_bf[c][:, :, j],
+                    in_=b_banks[c][:, CHUNK * j : CHUNK * (j + 1)],
+                    func=ACT.Copy,
+                    scale=weights[:, 1, j : j + 1],
+                )
+
+        def quantise(codes, plane, first, values):
+            width = values.shape[1] // PACK
+            nc.vector.quantize_mx(
+                out=codes[:, first : first + width].bitcast(FP8X4),
+                scales=plane[:, first : first + width],
+                in_=values,
+            )
+
+        def stored_passes(c):
+            for r in range(PACK):
+                nc.tensor.matmul_mx(
+                    out=v_banks[c][:, CHUNK * r : CHUNK * (r + 1)],
+                    lhsT=sa_codes[:, P * r : P * (r + 1)].bitcast(FP8X4),
+                    lhsT_scale=sa_plane[:, P * r : P * (r + 1)],
+                    rhs=sb_codes[:, 2 * CHUNK * c : 2 * CHUNK * (c + 1)].bitcast(FP4X4),
+                    rhs_scale=sb_plane[:, 0, CHUNK * c : CHUNK * (c + 1)],
+                    start=(r == 0),
+                    stop=False,
+                )
+
+        def token_passes(c):
+            for r in range(PACK):
+                nc.tensor.matmul_mx(
+                    out=v_banks[c][:, CHUNK * r : CHUNK * (r + 1)],
+                    lhsT=at_codes[:, P * r : P * (r + 1)].bitcast(FP8X4),
+                    lhsT_scale=at_plane[:, P * r : P * (r + 1)],
+                    rhs=bt_codes[:, CHUNK * c : CHUNK * (c + 1)].bitcast(FP8X4),
+                    rhs_scale=bt_plane[:, CHUNK * c : CHUNK * (c + 1)],
+                    start=False,
+                    stop=(r == PACK - 1),
+                )
+
+        out_rows = out_0.rearrange("(p r) m -> p r m", r=PACK)
+
+        def result_f32(c):
+            nc.scalar.mul(out=y_f32[c][:].rearrange("p r m -> p (r m)"), in_=v_banks[c][:], mul=OUT_SCALE)
+            nc.sync.dma_start(out=out_rows[:, :, CHUNK * c : CHUNK * (c + 1)], in_=y_f32[c][:])
+
+        def result_bf_from_sbuf(c):
+            nc.vector.tensor_copy(out=y_bf[c][:], in_=y_f32[c][:].rearrange("p r m -> p m r"))
+
+        def flat(tile):
+            return tile[:].rearrange("p c t -> p (c t)")
+
+        def result_planes(c):
+            quantise(y_codes, y_plane, CHUNK * c, flat(y_bf[c]))
+
+        def quantise_bt(c):
+            quantise(bt_codes, bt_plane, CHUNK * c, flat(bt_bf[c]))
+
+        def moment(c):
+            stored_passes(c)
+            token_passes(c)
+            result_f32(c)
+
+        nc.vector.tensor_copy(
+            out=sa_codes[:].bitcast(I32).rearrange("p (r h l) -> p h r l", r=PACK, l=4),
+            in_=sa_raw[:].bitcast(I32).rearrange("p (h l r) -> p h r l", r=PACK, l=4),
+        )
+        nc.vector.tensor_copy(out=weights[:], in_=weight_cols[:].rearrange("p (j s) -> p s j", s=8)[:, 0:2, :])
+        a_chunk(0)
+        nc.vector.tensor_copy(
+            out=sa_plane[:].rearrange("p (r h l) -> p h r l", r=PACK, l=16),
+            in_=sa_raw_plane[:, 0, :].rearrange("p (h l r) -> p h r l", r=PACK, l=16),
+        )
+        a_chunk(1)
+        a_chunk(2)
+        a_chunk(3)
+        b_matmuls(1)
+        b_weigh_on_scalar(1)
+        b_matmuls(0)
+        b_matmuls(2)
+        b_matmuls(3)
+        quantise(at_codes, at_plane, 0, at_bf[:].rearrange("p r c t -> p (r c t)"))
+        b_weigh_on_vector(0)
+        b_weigh_on_vector(2)
+        quantise_bt(0)
+        quantise_bt(1)
+        b_weigh_on_vector(3)
+        quantise_bt(2)
+        moment(0)
+        moment(1)
+        moment(2)
+        result_bf_from_sbuf(0)
+        quantise_bt(3)
+        moment(3)
+        result_bf_from_sbuf(1)
+        result_planes(0)
+        result_bf_from_sbuf(2)
+        result_planes(1)
+        result_planes(2)
+        out_words = out_1[0].rearrange("p c t -> p (c t)").bitcast(I32)
+        nc.sync.dma_start(out=out_words[:, : 3 * CHUNK], in_=y_codes[:, : 3 * CHUNK].bitcast(I32))
+        result_bf_from_sbuf(3)
+        result_planes(3)
+        nc.sync.dma_start(out=out_words[:, 3 * CHUNK :], in_=y_codes[:, 3 * CHUNK :].bitcast(I32))
+        for q in range(4):
+            queue = nc.scalar if q % 2 == 0 else nc.sync
+            queue.dma_start(
+                out=out_2[0, 4 * q : 4 * q + 4, :].bitcast(I32),
+                in_=y_plane[32 * q : 32 * q + 4, :].bitcast(I32),
+            )

@@ -20,6 +20,7 @@ PACK = 4
 PASSES = 2
 CHUNK = 128
 OUT_SCALE = 0.04
+WARM_PASSES = 24
 
 
 def tile_mix_moment_of_two_layers_pl_kernel(
@@ -91,9 +92,24 @@ def tile_mix_moment_of_two_layers_pl_kernel(
             words = wa_words.rearrange("g p c t -> p g (c t)").bitcast(I32)
             nc.sync.dma_start(out=wa_codes[h][:].bitcast(I32), in_=words[:, :, 256 * h : 256 * (h + 1)])
 
+        warm_bf = sbuf("warm_bf", [P, PACK * CHUNK], BF16)
+        warm_codes = sbuf("warm_codes", [P, CHUNK], U32)
+        warm_plane = sbuf("warm_plane", [P, CHUNK], U8)
         nc.vector.memset(weight_rows[:], 0.0)
+        nc.vector.memset(warm_bf[:].bitcast(I32), 0)
         for plane in (sa_raw_plane, wa_plane):
             zero_plane(plane)
+        nc.vector.quantize_mx(out=warm_codes[:].bitcast(FP8X4), scales=warm_plane[:], in_=warm_bf[:])
+        for i in range(WARM_PASSES):
+            nc.tensor.matmul_mx(
+                out=b_banks[3][:, CHUNK * (i % 4) : CHUNK * (i % 4 + 1)],
+                lhsT=warm_codes[:].bitcast(FP8X4),
+                lhsT_scale=warm_plane[:],
+                rhs=warm_codes[:].bitcast(FP8X4),
+                rhs_scale=warm_plane[:],
+                start=True,
+                stop=True,
+            )
         for g in range(PASSES):
             nc.vector.memset(xt_plane[g][:].bitcast(I32), 0)
         for plane in (wb_plane, sb_plane):

@@ -82,8 +82,8 @@ def tile_mix_moment_of_two_layers_pl_kernel(
             for q in range(4):
                 load_scale_rows(nc.sync if q % 2 == 0 else nc.scalar, plane, scales, q)
 
-        def load_weight_row(row, vector):
-            nc.scalar.dma_start(
+        def load_weight_row(queue, row, vector):
+            queue.dma_start(
                 out=weight_rows[row:P:8, :].rearrange("u (q i) -> u q i", i=8),
                 in_=vector.rearrange("o (q u i) -> u (o q) i", u=16, i=8),
             )
@@ -95,10 +95,9 @@ def tile_mix_moment_of_two_layers_pl_kernel(
         warm_bf = sbuf("warm_bf", [P, PACK * CHUNK], BF16)
         warm_codes = sbuf("warm_codes", [P, CHUNK], U32)
         warm_plane = sbuf("warm_plane", [P, CHUNK], U8)
-        nc.vector.memset(weight_rows[:], 0.0)
+        zero_plane(wa_plane)
         nc.vector.memset(warm_bf[:].bitcast(I32), 0)
-        for plane in (sa_raw_plane, wa_plane):
-            zero_plane(plane)
+        nc.vector.memset(weight_rows[:], 0.0)
         nc.vector.quantize_mx(out=warm_codes[:].bitcast(FP8X4), scales=warm_plane[:], in_=warm_bf[:])
         for i in range(WARM_PASSES):
             nc.tensor.matmul_mx(
@@ -112,26 +111,28 @@ def tile_mix_moment_of_two_layers_pl_kernel(
             )
         for g in range(PASSES):
             nc.vector.memset(xt_plane[g][:].bitcast(I32), 0)
-        for plane in (wb_plane, sb_plane):
+        for plane in (wb_plane, sa_raw_plane, sb_plane):
             zero_plane(plane)
 
         load_plane(xt_raw_plane, xt_scales)
         nc.sync.dma_start(out=xt_raw[:].bitcast(I32), in_=xt_words.rearrange("g p c -> p g c").bitcast(I32))
+        load_scale_rows(nc.scalar, wa_plane, wa_scales, 0)
         load_wa_half(0)
-        load_weight_row(0, ra)
-        load_weight_row(1, rb)
-        for q in range(2, 4):
-            load_scale_rows(nc.gpsimd, sa_raw_plane, sa_scales, q)
-        load_plane(wa_plane, wa_scales)
+        load_scale_rows(nc.scalar, wa_plane, wa_scales, 1)
+        load_scale_rows(nc.sync, wa_plane, wa_scales, 2)
+        load_scale_rows(nc.scalar, wa_plane, wa_scales, 3)
+        load_weight_row(nc.sync, 0, ra)
+        load_weight_row(nc.scalar, 1, rb)
         load_wa_half(1)
         nc.sync.dma_start(out=sa_raw[:].bitcast(I32), in_=sa_words[0].rearrange("p c t -> p (c t)").bitcast(I32))
-        for q in range(2):
-            load_scale_rows(nc.scalar, sa_raw_plane, sa_scales, q)
-        load_plane(wb_plane, wb_scales)
+        for q in range(4):
+            load_scale_rows(nc.sync, wb_plane, wb_scales, q)
         nc.sync.dma_start(out=wb_codes[:].bitcast(I32), in_=wb_words.rearrange("g p c -> p g c").bitcast(I32))
+        for q in range(4):
+            load_scale_rows(nc.sync, sa_raw_plane, sa_scales, q)
         nc.sync.dma_start(out=sb_codes[:].bitcast(I32), in_=sb_words[0].bitcast(I32))
         for q in range(4):
-            load_scale_rows(nc.scalar if q < 2 else nc.sync, sb_plane, sb_scales, q)
+            load_scale_rows(nc.sync, sb_plane, sb_scales, q)
 
         for g in range(PASSES):
             for q in range(4):
@@ -252,23 +253,22 @@ def tile_mix_moment_of_two_layers_pl_kernel(
             quantise(bt_codes, bt_plane, CHUNK * c, flat(bt_bf[c]))
 
         def moment(c):
-            stored_passes(c)
             token_passes(c)
             result_f32(c)
 
+        nc.vector.tensor_copy(out=weights[:], in_=weight_cols[:].rearrange("p (j s) -> p s j", s=8)[:, 0:2, :])
+        a_chunk(0)
         nc.vector.tensor_copy(
             out=sa_codes[:].bitcast(I32).rearrange("p (r h l) -> p h r l", r=PACK, l=4),
             in_=sa_raw[:].bitcast(I32).rearrange("p (h l r) -> p h r l", r=PACK, l=4),
         )
-        nc.vector.tensor_copy(out=weights[:], in_=weight_cols[:].rearrange("p (j s) -> p s j", s=8)[:, 0:2, :])
-        a_chunk(0)
+        a_chunk(1)
+        a_chunk(2)
+        a_chunk(3)
         nc.vector.tensor_copy(
             out=sa_plane[:].rearrange("p (r h l) -> p h r l", r=PACK, l=16),
             in_=sa_raw_plane[:, 0, :].rearrange("p (h l r) -> p h r l", r=PACK, l=16),
         )
-        a_chunk(1)
-        a_chunk(2)
-        a_chunk(3)
         b_matmuls(1)
         b_weigh_on_scalar(1)
         b_matmuls(0)
@@ -281,12 +281,16 @@ def tile_mix_moment_of_two_layers_pl_kernel(
         quantise_bt(1)
         b_weigh_on_vector(3)
         quantise_bt(2)
+        quantise_bt(3)
+        stored_passes(0)
+        stored_passes(1)
         moment(0)
         moment(1)
+        stored_passes(2)
         moment(2)
-        result_bf_from_sbuf(0)
-        quantise_bt(3)
+        stored_passes(3)
         moment(3)
+        result_bf_from_sbuf(0)
         result_bf_from_sbuf(1)
         result_planes(0)
         result_bf_from_sbuf(2)

@@ -124,10 +124,10 @@ def tile_mix_moment_of_two_layers_pl_kernel(
         load_weight_row(nc.sync, 0, ra)
         load_weight_row(nc.scalar, 1, rb)
         load_wa_half(1)
-        nc.sync.dma_start(out=sa_raw[:].bitcast(I32), in_=sa_words[0].rearrange("p c t -> p (c t)").bitcast(I32))
+        nc.sync.dma_start(out=wb_codes[:].bitcast(I32), in_=wb_words.rearrange("g p c -> p g c").bitcast(I32))
         for q in range(4):
             load_scale_rows(nc.sync, wb_plane, wb_scales, q)
-        nc.sync.dma_start(out=wb_codes[:].bitcast(I32), in_=wb_words.rearrange("g p c -> p g c").bitcast(I32))
+        nc.sync.dma_start(out=sa_raw[:].bitcast(I32), in_=sa_words[0].rearrange("p c t -> p (c t)").bitcast(I32))
         for q in range(4):
             load_scale_rows(nc.sync, sa_raw_plane, sa_scales, q)
         nc.sync.dma_start(out=sb_codes[:].bitcast(I32), in_=sb_words[0].bitcast(I32))
@@ -257,50 +257,48 @@ def tile_mix_moment_of_two_layers_pl_kernel(
             result_f32(c)
 
         nc.vector.tensor_copy(out=weights[:], in_=weight_cols[:].rearrange("p (j s) -> p s j", s=8)[:, 0:2, :])
-        a_chunk(0)
+        out_words = out_1[0].rearrange("p c t -> p (c t)").bitcast(I32)
+
+        def store_words(h):
+            columns = slice(2 * CHUNK * h, 2 * CHUNK * (h + 1))
+            nc.sync.dma_start(out=out_words[:, columns], in_=y_codes[:, columns].bitcast(I32))
+
+        for c in range(4):
+            a_chunk(c)
+        b_matmuls(1)
+        b_weigh_on_scalar(1)
+        for c in (0, 2, 3):
+            b_matmuls(c)
         nc.vector.tensor_copy(
             out=sa_codes[:].bitcast(I32).rearrange("p (r h l) -> p h r l", r=PACK, l=4),
             in_=sa_raw[:].bitcast(I32).rearrange("p (h l r) -> p h r l", r=PACK, l=4),
         )
-        a_chunk(1)
-        a_chunk(2)
-        a_chunk(3)
+        quantise(at_codes, at_plane, 0, at_bf[:].rearrange("p r c t -> p (r c t)"))
+        b_weigh_on_vector(0)
         nc.vector.tensor_copy(
             out=sa_plane[:].rearrange("p (r h l) -> p h r l", r=PACK, l=16),
             in_=sa_raw_plane[:, 0, :].rearrange("p (h l r) -> p h r l", r=PACK, l=16),
         )
-        b_matmuls(1)
-        b_weigh_on_scalar(1)
-        b_matmuls(0)
-        b_matmuls(2)
-        b_matmuls(3)
-        quantise(at_codes, at_plane, 0, at_bf[:].rearrange("p r c t -> p (r c t)"))
-        b_weigh_on_vector(0)
-        b_weigh_on_vector(2)
         quantise_bt(0)
+        b_weigh_on_vector(2)
         quantise_bt(1)
         b_weigh_on_vector(3)
         quantise_bt(2)
         quantise_bt(3)
-        stored_passes(0)
-        stored_passes(1)
-        moment(0)
-        moment(1)
-        stored_passes(2)
-        moment(2)
-        stored_passes(3)
-        moment(3)
-        result_bf_from_sbuf(0)
-        result_bf_from_sbuf(1)
-        result_planes(0)
+        for c in range(4):
+            stored_passes(c)
+            moment(c)
+            if c == 1:
+                result_bf_from_sbuf(0)
+                result_bf_from_sbuf(1)
+                result_planes(0)
+                result_planes(1)
+        store_words(0)
         result_bf_from_sbuf(2)
-        result_planes(1)
-        result_planes(2)
-        out_words = out_1[0].rearrange("p c t -> p (c t)").bitcast(I32)
-        nc.sync.dma_start(out=out_words[:, : 3 * CHUNK], in_=y_codes[:, : 3 * CHUNK].bitcast(I32))
         result_bf_from_sbuf(3)
+        result_planes(2)
         result_planes(3)
-        nc.sync.dma_start(out=out_words[:, 3 * CHUNK :], in_=y_codes[:, 3 * CHUNK :].bitcast(I32))
+        store_words(1)
         for q in range(4):
             queue = nc.scalar if q % 2 == 0 else nc.sync
             queue.dma_start(

from contextlib import ExitStack

import concourse.mybir as mybir

K, T, S, N, M = 1024, 512, 512, 512, 512
FLOPS = 2 * K * T * (N + M) + 2 * (T + S) * N * M

F32 = mybir.dt.float32
BF16 = mybir.dt.bfloat16
I32 = mybir.dt.int32
U32 = mybir.dt.uint32
U8 = mybir.dt.uint8
FP8X4 = mybir.dt.float8_e4m3fn_x4
FP4X4 = mybir.dt.float4_e2m1fn_x4
ALU = mybir.AluOpType
ACT = mybir.ActivationFunctionType

P = 128
PACK = 4
PASSES = 2
CHUNK = 128
OUT_SCALE = 0.04
WARM_PASSES = 24


def tile_mix_moment_of_two_layers_pl_kernel(
    tc, xt_words, xt_scales, wa_words, wa_scales, wb_words, wb_scales, ra, rb,
    sa_words, sa_scales, sb_words, sb_scales, out_0, out_1, out_2,
):
    nc = tc.nc
    with ExitStack() as ctx:
        sb = ctx.enter_context(tc.tile_pool(name="sb", bufs=1))
        ps = ctx.enter_context(tc.psum_pool(name="ps", bufs=1))
        ctx.enter_context(tc.manual_schedule())

        def sbuf(name, shape, dtype):
            return sb.tile(shape, dtype, name=name, align_bytes=64)

        banks = [ps.tile([P, 512], F32, name="bank%d" % i) for i in range(8)]
        a_banks = banks[0:4]
        b_banks = banks[4:8]
        v_banks = banks[0:4]

        xt_raw = sbuf("xt_raw", [P, PASSES, 2 * T], U8)
        xt_raw_plane = sbuf("xt_raw_plane", [P, PASSES, T], U8)
        xt_codes = [sbuf("xt_codes%d" % g, [P, 2 * T], U8) for g in range(PASSES)]
        xt_plane = [sbuf("xt_plane%d" % g, [P, T], U8) for g in range(PASSES)]
        wa_codes = [sbuf("wa_codes%d" % h, [P, PASSES, N // 2], U32) for h in range(2)]
        wa_plane = sbuf("wa_plane", [P, PASSES, N], U8)
        wb_codes = sbuf("wb_codes", [P, PASSES, 2 * M], U8)
        wb_plane = sbuf("wb_plane", [P, PASSES, M], U8)
        sa_raw = sbuf("sa_raw", [P, N], U32)
        sa_raw_plane = sbuf("sa_raw_plane", [P, 1, N], U8)
        sa_codes = sbuf("sa_codes", [P, N], U32)
        sa_plane = sbuf("sa_plane", [P, N], U8)
        sb_codes = sbuf("sb_codes", [P, 2 * M], U8)
        sb_plane = sbuf("sb_plane", [P, 1, M], U8)
        weight_rows = sbuf("weight_rows", [P, 32], F32)
        weight_cols = sbuf("weight_cols", [P, 32], F32)
        weights = sbuf("weights", [P, 2, PACK], F32)
        at_bf = sbuf("at_bf", [P, PACK, P, PACK], BF16)
        at_codes = sbuf("at_codes", [P, N], U32)
        at_plane = sbuf("at_plane", [P, N], U8)
        bt_bf = [sbuf("bt_bf%d" % c, [P, CHUNK, PACK], BF16) for c in range(4)]
        bt_codes = sbuf("bt_codes", [P, M], U32)
        bt_plane = sbuf("bt_plane", [P, M], U8)
        y_f32 = [sbuf("y_f32_%d" % c, [P, PACK, CHUNK], F32) for c in range(4)]
        y_bf = [sbuf("y_bf%d" % c, [P, CHUNK, PACK], BF16) for c in range(4)]
        y_codes = sbuf("y_codes", [P, M], U32)
        y_plane = sbuf("y_plane", [P, M], U8)

        def zero_plane(plane):
            nc.vector.memset(plane[:].rearrange("p g c -> p (g c)").bitcast(I32), 0)

        def load_scale_rows(queue, plane, scales, q):
            queue.dma_start(
                out=plane[32 * q : 32 * q + 4, :, :].bitcast(I32),
                in_=scales.bitcast(I32)[:, 4 * q : 4 * q + 4, :].rearrange("g r c -> r g c"),
            )

        def load_plane(plane, scales):
            for q in range(4):
                load_scale_rows(nc.sync if q % 2 == 0 else nc.scalar, plane, scales, q)

        def load_weight_row(queue, row, vector):
            queue.dma_start(
                out=weight_rows[row:P:8, :].rearrange("u (q i) -> u q i", i=8),
                in_=vector.rearrange("o (q u i) -> u (o q) i", u=16, i=8),
            )

        def load_wa_half(h):
            words = wa_words.rearrange("g p c t -> p g (c t)").bitcast(I32)
            nc.sync.dma_start(out=wa_codes[h][:].bitcast(I32), in_=words[:, :, 256 * h : 256 * (h + 1)])

        warm_bf = sbuf("warm_bf", [P, PACK * CHUNK], BF16)
        warm_codes = sbuf("warm_codes", [P, CHUNK], U32)
        warm_plane = sbuf("warm_plane", [P, CHUNK], U8)
        zero_plane(wa_plane)
        nc.vector.memset(warm_bf[:].bitcast(I32), 0)
        nc.vector.memset(weight_rows[:], 0.0)
        nc.vector.quantize_mx(out=warm_codes[:].bitcast(FP8X4), scales=warm_plane[:], in_=warm_bf[:])
        for i in range(WARM_PASSES):
            nc.tensor.matmul_mx(
                out=b_banks[3][:, CHUNK * (i % 4) : CHUNK * (i % 4 + 1)],
                lhsT=warm_codes[:].bitcast(FP8X4),
                lhsT_scale=warm_plane[:],
                rhs=warm_codes[:].bitcast(FP8X4),
                rhs_scale=warm_plane[:],
                start=True,
                stop=True,
            )
        for g in range(PASSES):
            nc.vector.memset(xt_plane[g][:].bitcast(I32), 0)
        for plane in (wb_plane, sa_raw_plane, sb_plane):
            zero_plane(plane)

        load_plane(xt_raw_plane, xt_scales)
        nc.sync.dma_start(out=xt_raw[:].bitcast(I32), in_=xt_words.rearrange("g p c -> p g c").bitcast(I32))
        load_scale_rows(nc.scalar, wa_plane, wa_scales, 0)
        load_wa_half(0)
        load_scale_rows(nc.scalar, wa_plane, wa_scales, 1)
        load_scale_rows(nc.sync, wa_plane, wa_scales, 2)
        load_scale_rows(nc.scalar, wa_plane, wa_scales, 3)
        load_weight_row(nc.sync, 0, ra)
        load_weight_row(nc.scalar, 1, rb)
        load_wa_half(1)
        nc.sync.dma_start(out=wb_codes[:].bitcast(I32), in_=wb_words.rearrange("g p c -> p g c").bitcast(I32))
        for q in range(4):
            load_scale_rows(nc.sync, wb_plane, wb_scales, q)
        nc.sync.dma_start(out=sa_raw[:].bitcast(I32), in_=sa_words[0].rearrange("p c t -> p (c t)").bitcast(I32))
        for q in range(4):
            load_scale_rows(nc.sync, sa_raw_plane, sa_scales, q)
        nc.sync.dma_start(out=sb_codes[:].bitcast(I32), in_=sb_words[0].bitcast(I32))
        for q in range(4):
            load_scale_rows(nc.sync, sb_plane, sb_scales, q)

        for g in range(PASSES):
            for q in range(4):
                rows = slice(32 * q, 32 * q + 4)
                nc.vector.tensor_copy(
                    out=xt_plane[g][rows, :].bitcast(I32).rearrange("p (j b q w) -> p j b q w", j=4, b=4, q=4),
                    in_=xt_raw_plane[rows, g, :].bitcast(I32).rearrange("p (q b j w) -> p j b q w", q=4, b=4, j=4),
                )
        for g in range(PASSES):
            nc.vector.tensor_copy(
                out=xt_codes[g][:].bitcast(I32).rearrange("p (j b q w) -> p j b q w", j=4, b=4, q=4),
                in_=xt_raw[:, g, :].bitcast(I32).rearrange("p (q b j w) -> p j b q w", q=4, b=4, j=4),
            )
        nc.vector.transpose(out=weight_cols[:], in_=weight_rows[:])

        def layer_group(out, j, codes_of, plane, first, width):
            for g in range(PASSES):
                nc.tensor.matmul_mx(
                    out=out,
                    lhsT=xt_codes[g][:, 2 * P * j : 2 * P * (j + 1)].bitcast(FP4X4),
                    lhsT_scale=xt_plane[g][:, P * j : P * (j + 1)],
                    rhs=codes_of(g, first, width),
                    rhs_scale=plane[:, g, first : first + width],
                    start=(g == 0),
                    stop=(g == PASSES - 1),
                )

        def wa_view(g, first, width):
            h, column = divmod(first, N // 2)
            return wa_codes[h][:, g, column : column + width].bitcast(FP8X4)

        def wb_view(g, first, width):
            return wb_codes[:, g, 2 * first : 2 * (first + width)].bitcast(FP4X4)

        def a_chunk(c):
            for j in range(PACK):
                layer_group(a_banks[c][:, CHUNK * j : CHUNK * (j + 1)], j, wa_view, wa_plane, CHUNK * c, CHUNK)
            sums = a_banks[c][:].rearrange("p (j q r) -> p r q j", j=PACK, r=PACK)
            for r in range(PACK):
                nc.vector.scalar_tensor_tensor(
                    out=at_bf[:, r, 32 * c : 32 * (c + 1), :],
                    in0=sums[:, r, :, :],
                    scalar=0.0,
                    in1=weights[:, 0:1, :].to_broadcast([P, 32, PACK]),
                    op0=ALU.max,
                    op1=ALU.mult,
                )

        def b_matmuls(c):
            for j in range(PACK):
                layer_group(b_banks[c][:, CHUNK * j : CHUNK * (j + 1)], j, wb_view, wb_plane, CHUNK * c, CHUNK)

        def b_weigh_on_vector(c):
            nc.vector.tensor_tensor(
                out=bt_bf[c][:],
                in0=b_banks[c][:].rearrange("p (j m) -> p m j", j=PACK),
                in1=weights[:, 1:2, :].to_broadcast([P, CHUNK, PACK]),
                op=ALU.mult,
            )

        def b_weigh_on_scalar(c):
            for j in range(PACK):
                nc.scalar.activation(
                    out=bt_bf[c][:, :, j],
                    in_=b_banks[c][:, CHUNK * j : CHUNK * (j + 1)],
                    func=ACT.Copy,
                    scale=weights[:, 1, j : j + 1],
                )

        def quantise(codes, plane, first, values):
            width = values.shape[1] // PACK
            nc.vector.quantize_mx(
                out=codes[:, first : first + width].bitcast(FP8X4),
                scales=plane[:, first : first + width],
                in_=values,
            )

        def stored_passes(c):
            for r in range(PACK):
                nc.tensor.matmul_mx(
                    out=v_banks[c][:, CHUNK * r : CHUNK * (r + 1)],
                    lhsT=sa_codes[:, P * r : P * (r + 1)].bitcast(FP8X4),
                    lhsT_scale=sa_plane[:, P * r : P * (r + 1)],
                    rhs=sb_codes[:, 2 * CHUNK * c : 2 * CHUNK * (c + 1)].bitcast(FP4X4),
                    rhs_scale=sb_plane[:, 0, CHUNK * c : CHUNK * (c + 1)],
                    start=(r == 0),
                    stop=False,
                )

        def token_passes(c):
            for r in range(PACK):
                nc.tensor.matmul_mx(
                    out=v_banks[c][:, CHUNK * r : CHUNK * (r + 1)],
                    lhsT=at_codes[:, P * r : P * (r + 1)].bitcast(FP8X4),
                    lhsT_scale=at_plane[:, P * r : P * (r + 1)],
                    rhs=bt_codes[:, CHUNK * c : CHUNK * (c + 1)].bitcast(FP8X4),
                    rhs_scale=bt_plane[:, CHUNK * c : CHUNK * (c + 1)],
                    start=False,
                    stop=(r == PACK - 1),
                )

        out_rows = out_0.rearrange("(p r) m -> p r m", r=PACK)

        def result_f32(c):
            nc.scalar.mul(out=y_f32[c][:].rearrange("p r m -> p (r m)"), in_=v_banks[c][:], mul=OUT_SCALE)
            nc.sync.dma_start(out=out_rows[:, :, CHUNK * c : CHUNK * (c + 1)], in_=y_f32[c][:])

        def result_bf_from_sbuf(c):
            nc.vector.tensor_copy(out=y_bf[c][:], in_=y_f32[c][:].rearrange("p r m -> p m r"))

        def flat(tile):
            return tile[:].rearrange("p c t -> p (c t)")

        def result_planes(c):
            quantise(y_codes, y_plane, CHUNK * c, flat(y_bf[c]))

        def quantise_bt(c):
            quantise(bt_codes, bt_plane, CHUNK * c, flat(bt_bf[c]))

        def moment(c):
            token_passes(c)
            result_f32(c)

        nc.vector.tensor_copy(out=weights[:], in_=weight_cols[:].rearrange("p (j s) -> p s j", s=8)[:, 0:2, :])
        out_words = out_1[0].rearrange("p c t -> p (c t)").bitcast(I32)

        def store_words(h):
            columns = slice(2 * CHUNK * h, 2 * CHUNK * (h + 1))
            nc.sync.dma_start(out=out_words[:, columns], in_=y_codes[:, columns].bitcast(I32))

        for c in range(4):
            a_chunk(c)
        b_matmuls(1)
        b_weigh_on_scalar(1)
        for c in (0, 2, 3):
            b_matmuls(c)
        nc.vector.tensor_copy(
            out=sa_codes[:].bitcast(I32).rearrange("p (r h l) -> p h r l", r=PACK, l=4),
            in_=sa_raw[:].bitcast(I32).rearrange("p (h l r) -> p h r l", r=PACK, l=4),
        )
        quantise(at_codes, at_plane, 0, at_bf[:].rearrange("p r c t -> p (r c t)"))
        b_weigh_on_vector(0)
        nc.vector.tensor_copy(
            out=sa_plane[:].rearrange("p (r h l) -> p h r l", r=PACK, l=16),
            in_=sa_raw_plane[:, 0, :].rearrange("p (h l r) -> p h r l", r=PACK, l=16),
        )
        quantise_bt(0)
        b_weigh_on_vector(2)
        quantise_bt(1)
        b_weigh_on_vector(3)
        quantise_bt(2)
        quantise_bt(3)
        for c in range(4):
            stored_passes(c)
            moment(c)
            if c == 1:
                result_bf_from_sbuf(0)
                result_bf_from_sbuf(1)
                result_planes(0)
                result_planes(1)
        store_words(0)
        result_bf_from_sbuf(2)
        result_bf_from_sbuf(3)
        result_planes(2)
        result_planes(3)
        store_words(1)
        for q in range(4):
            queue = nc.scalar if q % 2 == 0 else nc.sync
            queue.dma_start(
                out=out_2[0, 4 * q : 4 * q + 4, :].bitcast(I32),
                in_=y_plane[32 * q : 32 * q + 4, :].bitcast(I32),
            )
